import numpy as np, ml_dtypes
CORES = [2,10,50,58,66,74,122]
N = 7
DEG, TK = 2, 256
MASK = [[0,1],[0,1],[0,2],[0,3],[0,4],[0,5],[0,6]]
def setup_inputs(rng):
    return {"x": rng.standard_normal((N, 128, TK), dtype=np.float32).astype(ml_dtypes.bfloat16), "w": rng.standard_normal((N, 128, DEG * 128), dtype=np.float32).astype(ml_dtypes.bfloat16)}
def setup_inputs_big(rng):
    d = setup_inputs(rng)
    for k in ("x", "w"): d[k] = (d[k].astype(np.float32) * 1024.0).astype(d[k].dtype)
    return d
def setup_inputs_small(rng):
    d = setup_inputs(rng)
    for k in ("x", "w"): d[k] = (d[k].astype(np.float32) * (1 / 1024.0)).astype(d[k].dtype)
    return d
def setup_inputs_apart(rng):
    d = setup_inputs(rng)
    f = (10.0 ** rng.permutation(np.linspace(-1.5, 1.5, N))).astype(np.float32).reshape(N, 1, 1)
    for k in ("x", "w"): d[k] = (d[k].astype(np.float32) * f).astype(d[k].dtype)
    return d
def reference(x, w):
    X, W = x.astype(np.float64), w.astype(np.float64)
    y = np.zeros((N, 128, TK))
    for r in range(N):
        for i, j in enumerate(MASK[r]):
            y[r] += W[r][:, 128 * i:128 * i + 128].T @ X[j]
    return {"y": y.astype(ml_dtypes.bfloat16 if x.dtype != np.float64 else np.float64)}

from concourse.bass import DstId, RemoteDMATransfer

P = 128
TK = 256
KEEP_FAR = 1

SCRATCH = {
    "xs": ("sbuf", [P, TK], "bfloat16"),
    "ws": ("sbuf", [P, 2 * P], "bfloat16"),
    "land0": ("sbuf", [P, TK], "bfloat16"),
    "land1": ("sbuf", [P, TK], "bfloat16"),
    "ys": ("sbuf", [P, TK], "bfloat16"),
    "ps": ("psum", [P, 512], "float32"),
}
SEMAPHORES = ["xl", "wl", "arr0", "arr1", "snt", "mm", "cp", "st"]


def _hops(topo, a, b):
    ca, cb = topo.chip(a), topo.chip(b)
    if ca == cb:
        return 0
    return 1 if (topo.mates(ca, cb) or topo.same_plane(ca, cb)) else 2


def _plan(T, topo):
    mask_t, cores = T.tables["MASK"], list(T.cores)
    own = {c: [] for c in cores}
    passed = {c: [] for c in cores}
    for j, src in enumerate(cores):
        cons = [(cores[r], mask_t[r].index(j)) for r in range(len(cores)) if r != j and j in mask_t[r]]
        for tile in sorted({t for _, t in cons}):
            dsts = [c for c, t in cons if t == tile]
            far = [c for c in dsts if _hops(topo, src, c) == 2]
            near = [c for c in dsts if _hops(topo, src, c) < 2]
            relays = [c for c in near if topo.mates(topo.chip(src), topo.chip(c))
                      and all(_hops(topo, c, f) == 1 and topo.may_write(c, f) for f in far)]
            if relays and len(far) > KEEP_FAR:
                relay = relays[0]
                own[src].append((None, tile, [relay]))
                rest = far[:KEEP_FAR] + [c for c in near if c != relay]
                if rest:
                    own[src].append((None, tile, rest))
                passed[relay].append((tile, tile, far[KEEP_FAR:]))
            else:
                own[src].append((None, tile, far + near))
    return own, passed


def _engines(m):
    return bin(m).count("1")


def rank_program(g, core, T, topo):
    rank = T.rank_of(core)
    if rank is None:
        return
    tiles = T.tables["MASK"][rank]
    own, passed = _plan(T, topo)
    land = [T.land0, T.land1]
    arr = [T.sem.arr0, T.sem.arr1]

    def arrival(tile):
        senders = [s for s in T.cores for table in (own, passed) for (_, t, ds) in table[s] if t == tile and core in ds]
        return _engines(topo.mask(senders[0], core))

    g.sync.dma_start(T.xs[:], T.x[:]).then_inc(T.sem.xl, 16)
    g.sync.dma_start(T.ws[:], T.w[:]).then_inc(T.sem.wl, 16)

    left = 0

    def send(src_ap, tile, dsts):
        m = topo.mask(core, dsts[0])
        for d in dsts:
            assert topo.may_write(core, d) and topo.mask(core, d) == m
        ids = [DstId(rid=topo.addr(d)[0], pnc=topo.addr(d)[1]) for d in dsts]
        g.remote_dma_fused(
            [RemoteDMATransfer(dst_ids=ids, dma_engine_mask=m, remote_sem=arr[tile],
                               srcs=[src_ap], dsts=[land[tile][:] for _ in dsts], alu_op=0)],
            local_sem=T.sem.snt)
        return _engines(m)

    if own[core]:
        g.wait_ge(T.sem.xl, 16)
        for _, tile, dsts in own[core]:
            left += send(T.xs[:], tile, dsts)
    for from_tile, tile, dsts in passed[core]:
        g.wait_ge(arr[from_tile], arrival(from_tile))
        left += send(land[from_tile][:], tile, dsts)

    order = sorted(range(len(tiles)), key=lambda i: tiles[i] != rank)
    g.tensor.wait_ge(T.sem.wl, 16)
    g.tensor.wait_ge(T.sem.xl, 16)
    for k, i in enumerate(order):
        if tiles[i] == rank:
            rhs = T.xs[:]
        else:
            g.tensor.wait_ge(arr[i], arrival(i))
            rhs = land[i][:]
        mm = g.tensor.matmul(T.ps[:, 0:TK], T.ws[:, i * P:(i + 1) * P], rhs, start=(k == 0), stop=(k == len(order) - 1))
    mm.then_inc(T.sem.mm, 1)

    g.vector.wait_ge(T.sem.mm, 1)
    g.vector.tensor_copy(T.ys[:], T.ps[:, 0:TK]).then_inc(T.sem.cp, 1)
    g.sync.wait_ge(T.sem.cp, 1)
    if left:
        g.sync.wait_ge(T.sem.snt, left)
    g.sync.dma_start(T.y[:], T.ys[:]).then_inc(T.sem.st, 16)
    g.sync.wait_ge(T.sem.st, 16)
